import numpy as np, ml_dtypes
CORES = [7,391,135,263,15,399,143,271]
N = 8
K, F = 2, 64
def setup_inputs(rng):
    return {"gr": rng.standard_normal((N, K, 128, N * F), dtype=np.float32).astype(ml_dtypes.bfloat16)}
def setup_inputs_big(rng):
    d = setup_inputs(rng)
    for k in ("gr",): d[k] = (d[k].astype(np.float32) * 1048576.0).astype(d[k].dtype)
    return d
def setup_inputs_small(rng):
    d = setup_inputs(rng)
    for k in ("gr",): d[k] = (d[k].astype(np.float32) * (1 / 1048576.0)).astype(d[k].dtype)
    return d
def reference(gr):
    s = gr.astype(np.float64).sum(axis=(0, 1))
    return {"y": np.stack([s[:, F * r:F * r + F] for r in range(N)]).astype(np.float32 if gr.dtype != np.float64 else np.float64)}

@@ -1,0 +1,95 @@
+from concourse.bass import DstId, RemoteDMATransfer
+from concourse.mybir import AluOpType
+
+N, K, F = 8, 2, 64
+W = N * F
+P2 = 2 * F
+
+SCRATCH = {
+    "tab": ("sbuf", [128, K * W], "bfloat16"),
+    "part": ("sbuf", [128, W], "float32"),
+    "land1": ("sbuf", [128, 3 * P2], "float32"),
+    "land2": ("sbuf", [128, F], "float32"),
+    "acc": ("sbuf", [128, 3 * F], "float32"),
+    "out": ("sbuf", [128, F], "float32"),
+}
+SEMAPHORES = ["loaded", "v0", "v1", "v2", "v3", "arr1", "arr2", "sent", "a0", "a1", "a2", "fin", "stored"]
+
+
+def rank_program(g, core, T, topo):
+    r = T.rank_of(core)
+    if r is None:
+        return
+    cores, S = T.cores, T.sem
+    add = AluOpType.add
+
+    def rack_of(c):
+        return topo.rack(topo.host(c))
+
+    def partner(q):
+        cq = cores[q]
+        return [p for p in range(N) if rack_of(cores[p]) != rack_of(cq) and topo.chip(cores[p]) == topo.chip(cq)
+                and topo.may_write(cq, cores[p])][0]
+
+    def kind(a, b):
+        return 2 if topo.mates(a, b) else (1 if topo.same_plane(a, b) else 0)
+
+    def piece(q):
+        p = partner(q)
+        assert abs(p - q) == 1
+        return F * min(p, q)
+
+    def engines(m):
+        return bin(m).count("1")
+
+    peers = sorted((q for q in range(N) if q != r and rack_of(cores[q]) == rack_of(core)),
+                   key=lambda q: kind(core, cores[q]))
+    p = partner(r)
+    mine, his = F * r - piece(r), F * p - piece(r)
+
+    g.sync.dma_start(T.tab[:, 0:W], T.gr[0]).then_inc(S.loaded, 16)
+    g.scalar.dma_start(T.tab[:, W:2 * W], T.gr[1]).then_inc(S.loaded, 16)
+
+    g.vector.wait_ge(S.loaded, 32)
+    for i, q in enumerate(peers + [r]):
+        lo = piece(q)
+        g.vector.tensor_tensor(T.part[:, lo:lo + P2], T.tab[:, lo:lo + P2], T.tab[:, W + lo:W + lo + P2],
+                               add).then_inc(S["v%d" % i], 1)
+
+    sent = landed = 0
+    for i, q in enumerate(peers):
+        lo, slot = piece(q), kind(core, cores[q])
+        rid, pid = topo.addr(cores[q], core)
+        m = topo.mask(core, cores[q])
+        g.wait_ge(S["v%d" % i], 1)
+        g.remote_dma(T.land1[:, slot * P2:(slot + 1) * P2], T.part[:, lo:lo + P2], S.arr1, S.sent, pid, rid, m)
+        sent += engines(m)
+        landed += engines(topo.mask(cores[q], core))
+
+    rid, pid = topo.addr(cores[p], core)
+    m = topo.mask(core, cores[p])
+    g.wait_ge(S.v3, 1)
+    g.wait_ge(S.arr1, landed)
+    g.remote_dma_fused([RemoteDMATransfer(
+        dst_ids=[DstId(rid=rid, pnc=pid)], dma_engine_mask=m, remote_sem=S.arr2,
+        srcs=[T.part[:, F * p:F * p + F]] + [T.land1[:, s * P2 + his:s * P2 + his + F] for s in range(3)],
+        dsts=[T.land2[:]], alu_op=1)], local_sem=S.sent)
+    sent += engines(m)
+
+    v = g.vector
+    v.wait_ge(S.v3, 1)
+    v.wait_ge(S.arr1, landed)
+    v.tensor_tensor(T.acc[:, 0:F], T.part[:, F * r:F * r + F], T.land1[:, mine:mine + F], add).then_inc(S.a0, 1)
+    v.tensor_tensor(T.acc[:, F:2 * F], T.land1[:, P2 + mine:P2 + mine + F],
+                    T.land1[:, 2 * P2 + mine:2 * P2 + mine + F], add).then_inc(S.a1, 1)
+    v.wait_ge(S.a0, 1)
+    v.wait_ge(S.a1, 1)
+    v.tensor_tensor(T.acc[:, 2 * F:3 * F], T.acc[:, 0:F], T.acc[:, F:2 * F], add).then_inc(S.a2, 1)
+    v.wait_ge(S.a2, 1)
+    v.wait_ge(S.arr2, engines(topo.mask(cores[p], core)))
+    v.tensor_tensor(T.out[:], T.acc[:, 2 * F:3 * F], T.land2[:], add).then_inc(S.fin, 1)
+
+    g.sync.wait_ge(S.fin, 1)
+    g.sync.dma_start(T.y[:], T.out[:]).then_inc(S.stored, 16)
+    g.sync.wait_ge(S.stored, 16)
+    g.wait_ge(S.sent, sent)

@@ -8,12 +8,15 @@ P2 = 2 * F
 SCRATCH = {
     "tab": ("sbuf", [128, K * W], "bfloat16"),
     "part": ("sbuf", [128, W], "float32"),
-    "land1": ("sbuf", [128, 3 * P2], "float32"),
+    "land1": ("sbuf", [128, 4 * F], "float32"),
+    "landf": ("sbuf", [128, 2 * F], "float32"),
     "land2": ("sbuf", [128, F], "float32"),
-    "acc": ("sbuf", [128, 3 * F], "float32"),
+    "acc": ("sbuf", [128, 2 * F], "float32"),
+    "accp": ("psum", [128, F], "float32"),
     "out": ("sbuf", [128, F], "float32"),
 }
-SEMAPHORES = ["loaded", "v0", "v1", "v2", "v3", "arr1", "arr2", "sent", "a0", "a1", "a2", "fin", "stored"]
+SEMAPHORES = ["loaded", "v0", "v1", "v2", "v3", "v4", "v5", "arr1", "arrf", "arr2", "sent", "a0", "a1", "a2", "fin",
+              "stored"]
 
 
 def rank_program(g, core, T, topo):
@@ -28,68 +31,79 @@ def rank_program(g, core, T, topo):
 
     def partner(q):
         cq = cores[q]
-        return [p for p in range(N) if rack_of(cores[p]) != rack_of(cq) and topo.chip(cores[p]) == topo.chip(cq)
-                and topo.may_write(cq, cores[p])][0]
-
-    def kind(a, b):
-        return 2 if topo.mates(a, b) else (1 if topo.same_plane(a, b) else 0)
+        return [x for x in range(N) if rack_of(cores[x]) != rack_of(cq) and topo.chip(cores[x]) == topo.chip(cq)
+                and topo.may_write(cq, cores[x])][0]
 
     def piece(q):
-        p = partner(q)
-        assert abs(p - q) == 1
-        return F * min(p, q)
+        x = partner(q)
+        assert abs(x - q) == 1
+        return F * min(x, q)
 
     def engines(m):
         return bin(m).count("1")
 
-    peers = sorted((q for q in range(N) if q != r and rack_of(cores[q]) == rack_of(core)),
-                   key=lambda q: kind(core, cores[q]))
+    rackers = [q for q in range(N) if q != r and rack_of(cores[q]) == rack_of(core)]
+    mate = [q for q in rackers if topo.mates(core, cores[q])][0]
+    plane = [q for q in rackers if topo.same_plane(core, cores[q])][0]
+    far = [q for q in rackers if q not in (mate, plane)][0]
     p = partner(r)
     mine, his = F * r - piece(r), F * p - piece(r)
 
     g.sync.dma_start(T.tab[:, 0:W], T.gr[0]).then_inc(S.loaded, 16)
     g.scalar.dma_start(T.tab[:, W:2 * W], T.gr[1]).then_inc(S.loaded, 16)
 
+    spans = [(F * partner(far), F), (F * partner(plane), F), (piece(mate), P2), (F * far, F), (F * plane, F),
+             (piece(r), P2)]
     g.vector.wait_ge(S.loaded, 32)
-    for i, q in enumerate(peers + [r]):
-        lo = piece(q)
-        g.vector.tensor_tensor(T.part[:, lo:lo + P2], T.tab[:, lo:lo + P2], T.tab[:, W + lo:W + lo + P2],
+    for i, (lo, n) in enumerate(spans):
+        g.vector.tensor_tensor(T.part[:, lo:lo + n], T.tab[:, lo:lo + n], T.tab[:, W + lo:W + lo + n],
                                add).then_inc(S["v%d" % i], 1)
 
-    sent = landed = 0
-    for i, q in enumerate(peers):
-        lo, slot = piece(q), kind(core, cores[q])
+    sent = [0]
+
+    def write(i, q, dst, sem):
+        lo, n = spans[i]
         rid, pid = topo.addr(cores[q], core)
         m = topo.mask(core, cores[q])
         g.wait_ge(S["v%d" % i], 1)
-        g.remote_dma(T.land1[:, slot * P2:(slot + 1) * P2], T.part[:, lo:lo + P2], S.arr1, S.sent, pid, rid, m)
-        sent += engines(m)
-        landed += engines(topo.mask(cores[q], core))
+        g.remote_dma(dst, T.part[:, lo:lo + n], sem, S.sent, pid, rid, m)
+        sent[0] += engines(m)
+
+    def lands(qs):
+        return sum(engines(topo.mask(cores[q], core)) for q in qs)
+
+    write(0, far, T.land1[:, 0:F], S.arr1)
+    write(1, plane, T.land1[:, F:2 * F], S.arr1)
+    write(2, mate, T.land1[:, 2 * F:4 * F], S.arr1)
+    write(3, far, T.landf[:, 0:F], S.arrf)
+    write(4, plane, T.landf[:, F:2 * F], S.arrf)
 
     rid, pid = topo.addr(cores[p], core)
     m = topo.mask(core, cores[p])
-    g.wait_ge(S.v3, 1)
-    g.wait_ge(S.arr1, landed)
+    g.wait_ge(S.v5, 1)
+    g.wait_ge(S.arr1, lands([far, plane, mate]))
     g.remote_dma_fused([RemoteDMATransfer(
         dst_ids=[DstId(rid=rid, pnc=pid)], dma_engine_mask=m, remote_sem=S.arr2,
-        srcs=[T.part[:, F * p:F * p + F]] + [T.land1[:, s * P2 + his:s * P2 + his + F] for s in range(3)],
+        srcs=[T.part[:, F * p:F * p + F], T.land1[:, 0:F], T.land1[:, F:2 * F],
+              T.land1[:, 2 * F + his:2 * F + his + F]],
         dsts=[T.land2[:]], alu_op=1)], local_sem=S.sent)
-    sent += engines(m)
+    sent[0] += engines(m)
 
     v = g.vector
-    v.wait_ge(S.v3, 1)
-    v.wait_ge(S.arr1, landed)
-    v.tensor_tensor(T.acc[:, 0:F], T.part[:, F * r:F * r + F], T.land1[:, mine:mine + F], add).then_inc(S.a0, 1)
-    v.tensor_tensor(T.acc[:, F:2 * F], T.land1[:, P2 + mine:P2 + mine + F],
-                    T.land1[:, 2 * P2 + mine:2 * P2 + mine + F], add).then_inc(S.a1, 1)
+    v.wait_ge(S.v5, 1)
+    v.wait_ge(S.arr1, lands([far, plane, mate]))
+    v.tensor_tensor(T.acc[:, 0:F], T.part[:, F * r:F * r + F], T.land1[:, 2 * F + mine:2 * F + mine + F],
+                    add).then_inc(S.a0, 1)
+    v.wait_ge(S.arrf, lands([far, plane]))
+    v.tensor_tensor(T.acc[:, F:2 * F], T.landf[:, 0:F], T.landf[:, F:2 * F], add).then_inc(S.a1, 1)
     v.wait_ge(S.a0, 1)
     v.wait_ge(S.a1, 1)
-    v.tensor_tensor(T.acc[:, 2 * F:3 * F], T.acc[:, 0:F], T.acc[:, F:2 * F], add).then_inc(S.a2, 1)
+    v.tensor_tensor(T.accp[:], T.acc[:, 0:F], T.acc[:, F:2 * F], add).then_inc(S.a2, 1)
     v.wait_ge(S.a2, 1)
-    v.wait_ge(S.arr2, engines(topo.mask(cores[p], core)))
-    v.tensor_tensor(T.out[:], T.acc[:, 2 * F:3 * F], T.land2[:], add).then_inc(S.fin, 1)
+    v.wait_ge(S.arr2, lands([p]))
+    v.tensor_tensor(T.out[:], T.accp[:], T.land2[:], add).then_inc(S.fin, 1)
 
     g.sync.wait_ge(S.fin, 1)
     g.sync.dma_start(T.y[:], T.out[:]).then_inc(S.stored, 16)
     g.sync.wait_ge(S.stored, 16)
-    g.wait_ge(S.sent, sent)
+    g.wait_ge(S.sent, sent[0])

from concourse.bass import DstId, RemoteDMATransfer
from concourse.mybir import AluOpType

N, K, F = 8, 2, 64
W = N * F
P2 = 2 * F

SCRATCH = {
    "tab": ("sbuf", [128, K * W], "bfloat16"),
    "part": ("sbuf", [128, W], "float32"),
    "land1": ("sbuf", [128, 4 * F], "float32"),
    "landf": ("sbuf", [128, 2 * F], "float32"),
    "land2": ("sbuf", [128, F], "float32"),
    "acc": ("sbuf", [128, 2 * F], "float32"),
    "accp": ("psum", [128, F], "float32"),
    "out": ("sbuf", [128, F], "float32"),
}
SEMAPHORES = ["loaded", "v0", "v1", "v2", "v3", "v4", "v5", "arr1", "arrf", "arr2", "sent", "a0", "a1", "a2", "fin",
              "stored"]


def rank_program(g, core, T, topo):
    r = T.rank_of(core)
    if r is None:
        return
    cores, S = T.cores, T.sem
    add = AluOpType.add

    def rack_of(c):
        return topo.rack(topo.host(c))

    def partner(q):
        cq = cores[q]
        return [x for x in range(N) if rack_of(cores[x]) != rack_of(cq) and topo.chip(cores[x]) == topo.chip(cq)
                and topo.may_write(cq, cores[x])][0]

    def piece(q):
        x = partner(q)
        assert abs(x - q) == 1
        return F * min(x, q)

    def engines(m):
        return bin(m).count("1")

    rackers = [q for q in range(N) if q != r and rack_of(cores[q]) == rack_of(core)]
    mate = [q for q in rackers if topo.mates(core, cores[q])][0]
    plane = [q for q in rackers if topo.same_plane(core, cores[q])][0]
    far = [q for q in rackers if q not in (mate, plane)][0]
    p = partner(r)
    mine, his = F * r - piece(r), F * p - piece(r)

    g.sync.dma_start(T.tab[:, 0:W], T.gr[0]).then_inc(S.loaded, 16)
    g.scalar.dma_start(T.tab[:, W:2 * W], T.gr[1]).then_inc(S.loaded, 16)

    spans = [(F * partner(far), F), (F * partner(plane), F), (piece(mate), P2), (F * far, F), (F * plane, F),
             (piece(r), P2)]
    g.vector.wait_ge(S.loaded, 32)
    for i, (lo, n) in enumerate(spans):
        g.vector.tensor_tensor(T.part[:, lo:lo + n], T.tab[:, lo:lo + n], T.tab[:, W + lo:W + lo + n],
                               add).then_inc(S["v%d" % i], 1)

    sent = [0]

    def write(i, q, dst, sem):
        lo, n = spans[i]
        rid, pid = topo.addr(cores[q], core)
        m = topo.mask(core, cores[q])
        g.wait_ge(S["v%d" % i], 1)
        g.remote_dma(dst, T.part[:, lo:lo + n], sem, S.sent, pid, rid, m)
        sent[0] += engines(m)

    def lands(qs):
        return sum(engines(topo.mask(cores[q], core)) for q in qs)

    write(0, far, T.land1[:, 0:F], S.arr1)
    write(1, plane, T.land1[:, F:2 * F], S.arr1)
    write(2, mate, T.land1[:, 2 * F:4 * F], S.arr1)
    write(3, far, T.landf[:, 0:F], S.arrf)
    write(4, plane, T.landf[:, F:2 * F], S.arrf)

    rid, pid = topo.addr(cores[p], core)
    m = topo.mask(core, cores[p])
    g.wait_ge(S.v5, 1)
    g.wait_ge(S.arr1, lands([far, plane, mate]))
    g.remote_dma_fused([RemoteDMATransfer(
        dst_ids=[DstId(rid=rid, pnc=pid)], dma_engine_mask=m, remote_sem=S.arr2,
        srcs=[T.part[:, F * p:F * p + F], T.land1[:, 0:F], T.land1[:, F:2 * F],
              T.land1[:, 2 * F + his:2 * F + his + F]],
        dsts=[T.land2[:]], alu_op=1)], local_sem=S.sent)
    sent[0] += engines(m)

    v = g.vector
    v.wait_ge(S.v5, 1)
    v.wait_ge(S.arr1, lands([far, plane, mate]))
    v.tensor_tensor(T.acc[:, 0:F], T.part[:, F * r:F * r + F], T.land1[:, 2 * F + mine:2 * F + mine + F],
                    add).then_inc(S.a0, 1)
    v.wait_ge(S.arrf, lands([far, plane]))
    v.tensor_tensor(T.acc[:, F:2 * F], T.landf[:, 0:F], T.landf[:, F:2 * F], add).then_inc(S.a1, 1)
    v.wait_ge(S.a0, 1)
    v.wait_ge(S.a1, 1)
    v.tensor_tensor(T.accp[:], T.acc[:, 0:F], T.acc[:, F:2 * F], add).then_inc(S.a2, 1)
    v.wait_ge(S.a2, 1)
    v.wait_ge(S.arr2, lands([p]))
    v.tensor_tensor(T.out[:], T.accp[:], T.land2[:], add).then_inc(S.fin, 1)

    g.sync.wait_ge(S.fin, 1)
    g.sync.dma_start(T.y[:], T.out[:]).then_inc(S.stored, 16)
    g.sync.wait_ge(S.stored, 16)
    g.wait_ge(S.sent, sent[0])
